import numpy as np
import ml_dtypes


def mxq(x, axis, fmt="e4m3"):
    dtype, down = {"e4m3": (ml_dtypes.float8_e4m3fn, 7), "e5m2": (ml_dtypes.float8_e5m2, 14)}[fmt]
    v = np.moveaxis(np.asarray(x, np.float32).astype(ml_dtypes.bfloat16).astype(np.float64), axis, -1)
    blocks = v.reshape(v.shape[:-1] + (-1, 32))
    amax = np.abs(blocks).max(-1, keepdims=True)
    byte = np.maximum(np.where(amax > 0, np.frexp(amax)[1] - 1 + 127, 0) - down, 1)
    scale = np.exp2(byte - 127.0)
    codes = (blocks / scale).astype(np.float32).astype(dtype).astype(np.float64)
    return np.moveaxis((codes * scale).reshape(v.shape), -1, axis)


WIDE = False


def mx_kscale(k):
    if not WIDE:
        return np.ones(k)
    levels = np.array([30, -30])
    if k % 512:
        return np.exp2(np.random.permutation(np.resize(levels, k // 32))).repeat(32)
    a = np.empty((k // 512, 16))
    for p in range(k // 512):
        a[p, :8] = np.random.permutation(np.resize(levels, 8))
        for g in range(8):
            far = levels[np.abs(levels - a[p, g]) >= 10]
            a[p, g + 8] = far[np.random.randint(len(far))]
    return np.exp2(a.ravel()).repeat(32)


def f64(x):
    return np.asarray(x).astype(np.float64)


def striped(idx):
    return np.tile(np.asarray(idx).reshape(-1, 16).T, (8, 1)).astype(np.uint16)


def unstriped(offs):
    return offs[:16].T.reshape(-1).astype(np.int64)


E2M1 = np.array([0.0, 0.5, 1.0, 1.5, 2.0, 3.0, 4.0, 6.0, -0.0, -0.5, -1.0, -1.5, -2.0, -3.0, -4.0, -6.0])


def pack_weight(w, fmt):
    k, n = w.shape
    w = f64(np.asarray(w, np.float32).astype(ml_dtypes.bfloat16)).reshape(k // 32, 32, n)
    amax = np.abs(w).max(1)
    if fmt == "e4m3":
        byte = np.frexp(amax)[1] - 1 + 127 - 7
    else:
        mant, ex = np.frexp(amax / 6.0)
        byte = np.where(mant > 0.5, ex, ex - 1) + 127
    byte = np.clip(np.where(amax > 0, byte, 1), 1, 254)
    scaled = (w * np.exp2(127.0 - byte)[:, None, :]).reshape(k, n).astype(np.float32)
    by_word = np.ascontiguousarray(scaled.reshape(k // 512, 128, 4, n).transpose(0, 1, 3, 2))
    if fmt == "e4m3":
        words = by_word.astype(ml_dtypes.float8_e4m3fn).view(np.uint8)
    else:
        c = by_word.astype(ml_dtypes.float4_e2m1fn).view(np.uint8) & 0xF
        words = (c[..., 0::2] | (c[..., 1::2] << 4)).reshape(k // 512, 128, 2 * n)
    return np.ascontiguousarray(words), np.ascontiguousarray(byte.astype(np.uint8).reshape(k // 512, 16, n))


def unpack_weight(words, scales, fmt):
    g, _, n = scales.shape
    words = np.ascontiguousarray(words).reshape(g, 128, n, -1)
    if fmt == "e4m3":
        vals = words.view(ml_dtypes.float8_e4m3fn).astype(np.float64)
    else:
        nib = np.empty((g, 128, n, 4), np.uint8)
        nib[..., 0::2] = words & 0xF
        nib[..., 1::2] = words >> 4
        vals = E2M1[nib]
    vals = vals * np.repeat(np.exp2(scales.astype(np.float64) - 127.0), 8, axis=1)[..., None]
    return vals.transpose(0, 1, 3, 2).reshape(g * 512, n)


def sigmoid(v):
    return 1.0 / (1.0 + np.exp(-v))


K, T, Z, J, R, Q, N = 512, 1024, 1024, 256, 512, 1024, 256


def setup_inputs():
    n = np.random.standard_normal
    idx = np.random.permutation(T)[:J]
    idx2 = np.random.permutation(Z)[:J]
    idx3 = np.random.permutation(Q)[:J]
    fk = mx_kscale(K)
    fr = mx_kscale(R)
    xtp = pack_weight(n((K, T)) / fk[:, None], "e2m1")
    xop = pack_weight(n((K, Z)) / fk[:, None], "e4m3")
    wp = pack_weight(n((K, R)) * 1 / np.sqrt(K) * fk[:, None] * fr, "e4m3")
    wbp = pack_weight(n((R, N)) * 1 / np.sqrt(R) / fr[:, None], "e2m1")
    return {
        "xt_words": xtp[0],
        "xt_scales": xtp[1],
        "xo_words": xop[0],
        "xo_scales": xop[1],
        "w_words": wp[0],
        "w_scales": wp[1],
        "tg": (1.0 * n((R, Q))).astype(np.float32),
        "sg": (np.random.uniform(0.6, 1.6, (R, 1))).astype(np.float32),
        "bg": (np.random.uniform(-1.0, 1.0, (R, 1))).astype(np.float32),
        "wb_words": wbp[0],
        "wb_scales": wbp[1],
        "offs": striped(idx),
        "offs2": striped(idx2),
        "offs3": striped(idx3),
    }


def reference(xt_words, xt_scales, xo_words, xo_scales, w_words, w_scales, tg, sg, bg, wb_words, wb_scales, offs, offs2, offs3):
    idx = unstriped(offs)
    idx2 = unstriped(offs2)
    idx3 = unstriped(offs3)
    xtu = unpack_weight(xt_words, xt_scales, "e2m1")
    xou = unpack_weight(xo_words, xo_scales, "e4m3")
    wu = unpack_weight(w_words, w_scales, "e4m3")
    wbu = unpack_weight(wb_words, wb_scales, "e2m1")
    xtidxg = xtu[:, idx]
    a = wu.T @ xtidxg
    xoidx2g = xou[:, idx2]
    b = wu.T @ xoidx2g
    hid = np.maximum(a, b) * sigmoid(f64(tg)[:, idx3] * f64(sg) + f64(bg))
    hidq = mxq(hid, 0, "e5m2")
    y = wbu.T @ hidq
    return y

@@ -1,0 +1,167 @@
+from contextlib import ExitStack
+
+import concourse.mybir as mybir
+
+K, T, J, R, N = 512, 1024, 256, 512, 256
+FLOPS = 2 * (2 * K * R * J) + 2 * R * N * J
+
+F32 = mybir.dt.float32
+BF16 = mybir.dt.bfloat16
+I32 = mybir.dt.int32
+U32 = mybir.dt.uint32
+U16 = mybir.dt.uint16
+U8 = mybir.dt.uint8
+E4M3 = mybir.dt.float8_e4m3fn_x4
+E5M2 = mybir.dt.float8_e5m2_x4
+E2M1 = mybir.dt.float4_e2m1fn_x4
+ALU = mybir.AluOpType
+ACT = mybir.ActivationFunctionType
+
+P = 128
+PACK = 4
+HALF = J // 2
+
+
+def load_scale_rows(queue, plane, scales):
+    for q in range(4):
+        queue.dma_start(
+            out=plane[32 * q : 32 * q + 4, :].bitcast(I32),
+            in_=scales[0, 4 * q : 4 * q + 4, :].bitcast(I32),
+        )
+
+
+def tile_list_oneforboth_tablegate_one_plain_kernel(
+    tc, xt_words, xt_scales, xo_words, xo_scales, w_words, w_scales, tg, sg, bg, wb_words, wb_scales, offs, offs2, offs3, out
+):
+    nc = tc.nc
+    with ExitStack() as ctx:
+        sb = ctx.enter_context(tc.tile_pool(name="sb", bufs=1))
+        ps = ctx.enter_context(tc.psum_pool(name="ps", bufs=1))
+
+        list_t = sb.tile([P, J // 16], U16, name="list_t")
+        list_o = sb.tile([P, J // 16], U16, name="list_o")
+        list_g = sb.tile([P, J // 16], U16, name="list_g")
+        xt_tab = sb.tile([P, T], U16, name="xt_tab", align_bytes=64)
+        xo_tab = sb.tile([P, T], U32, name="xo_tab", align_bytes=64)
+        xt_plane = sb.tile([P, T], U8, name="xt_plane", align_bytes=64)
+        xo_plane = sb.tile([P, T], U8, name="xo_plane", align_bytes=64)
+        w_raw = sb.tile([P, R], U32, name="w_raw", align_bytes=64)
+        w_plane = sb.tile([P, R], U8, name="w_plane", align_bytes=64)
+        wb_codes = sb.tile([P, 2 * N], U8, name="wb_codes", align_bytes=64)
+        wb_plane = sb.tile([P, N], U8, name="wb_plane", align_bytes=64)
+        slope = sb.tile([P, PACK], F32, name="slope")
+        offset = sb.tile([P, PACK], F32, name="offset")
+        tg_rows = [sb.tile([P, T], F32, name=f"tg_rows{t}", align_bytes=64) for t in range(PACK)]
+
+        for plane in (xt_plane, xo_plane, w_plane, wb_plane):
+            nc.vector.memset(plane[:].bitcast(I32), 0)
+
+        tg_by_t = tg.rearrange("(p t) q -> p t q", t=PACK)
+        nc.sync.dma_start(list_t[:], offs)
+        nc.sync.dma_start(out=xt_tab[:].bitcast(I32), in_=xt_words[0].bitcast(I32))
+        load_scale_rows(nc.scalar, xt_plane, xt_scales)
+        nc.sync.dma_start(out=w_raw[:].bitcast(I32), in_=w_words[0].rearrange("p c r -> p (c r)").bitcast(I32))
+        nc.sync.dma_start(out=xo_tab[:].bitcast(I32), in_=xo_words[0].rearrange("p c r -> p (c r)").bitcast(I32))
+        load_scale_rows(nc.scalar, w_plane, w_scales)
+        load_scale_rows(nc.gpsimd, xo_plane, xo_scales)
+        nc.sync.dma_start(list_o[:], offs2)
+        nc.sync.dma_start(out=tg_rows[0][:], in_=tg_by_t[:, 0, :])
+        nc.sync.dma_start(out=tg_rows[1][:], in_=tg_by_t[:, 1, :])
+        nc.sync.dma_start(list_g[:], offs3)
+        nc.scalar.dma_start(out=slope[:], in_=sg.rearrange("(p t) o -> p (t o)", t=PACK))
+        nc.scalar.dma_start(out=offset[:], in_=bg.rearrange("(p t) o -> p (t o)", t=PACK))
+        nc.sync.dma_start(out=tg_rows[2][:], in_=tg_by_t[:, 2, :])
+        nc.sync.dma_start(out=tg_rows[3][:], in_=tg_by_t[:, 3, :])
+        nc.sync.dma_start(out=wb_codes[:].bitcast(I32), in_=wb_words[0].bitcast(I32))
+        load_scale_rows(nc.sync, wb_plane, wb_scales)
+
+        xt_codes = sb.tile([P, J], U16, name="xt_codes", align_bytes=64)
+        xt_scale = sb.tile([P, J], U8, name="xt_scale", align_bytes=64)
+        xo_codes = sb.tile([P, J], U32, name="xo_codes", align_bytes=64)
+        xo_scale = sb.tile([P, J], U8, name="xo_scale", align_bytes=64)
+        w_codes = sb.tile([P, R], U32, name="w_codes", align_bytes=64)
+        w_scale = sb.tile([P, R], U8, name="w_scale", align_bytes=64)
+
+        nc.vector.tensor_copy(xt_codes[:], xt_tab[:].indirect(list_t[:]))
+        nc.vector.tensor_copy(xt_scale[:], xt_plane[:].indirect(list_t[:]))
+        nc.vector.tensor_copy(
+            out=w_codes[:].rearrange("p (t c i) -> p c t i", t=PACK, i=4),
+            in_=w_raw[:].rearrange("p (c i t) -> p c t i", t=PACK, i=4),
+        )
+        nc.vector.tensor_copy(
+            out=w_scale[:].rearrange("p (t c i) -> p c t i", t=PACK, i=16),
+            in_=w_plane[:].rearrange("p (c i t) -> p c t i", t=PACK, i=16),
+        )
+        nc.vector.tensor_copy(xo_codes[:], xo_tab[:].indirect(list_o[:]))
+        nc.vector.tensor_copy(xo_scale[:], xo_plane[:].indirect(list_o[:]))
+
+        gate = [sb.tile([P, 2, J], F32, name=f"gate{u}") for u in range(2)]
+
+        def look(t):
+            nc.scalar.activation(
+                out=gate[t // 2][:, t % 2, :],
+                in_=tg_rows[t][:].indirect(list_g[:]),
+                func=ACT.Sigmoid,
+                bias=offset[:, t : t + 1],
+                scale=slope[:, t : t + 1],
+            )
+
+        a_ps = [ps.tile([P, 2, J], F32, name=f"a_ps{u}") for u in range(2)]
+        b_ps = [ps.tile([P, 2, J], F32, name=f"b_ps{u}") for u in range(2)]
+        for acc, codes, scale in ((a_ps, xt_codes[:].bitcast(E2M1), xt_scale), (b_ps, xo_codes[:].bitcast(E4M3), xo_scale)):
+            for t in range(PACK):
+                cols = slice(P * t, P * (t + 1))
+                nc.tensor.matmul_mx(
+                    out=acc[t // 2][:, t % 2, :],
+                    lhsT=w_codes[:, cols].bitcast(E4M3),
+                    lhsT_scale=w_scale[:, cols],
+                    rhs=codes,
+                    rhs_scale=scale[:],
+                    start=True,
+                    stop=True,
+                )
+
+        hid = [sb.tile([P, HALF, PACK], BF16, name=f"hid{h}", align_bytes=64) for h in range(2)]
+        a_sb = [sb.tile([P, J, 2], F32, name=f"a_sb{u}") for u in range(2)]
+        top = [sb.tile([P, J, 2], F32, name=f"top{u}") for u in range(2)]
+        look(0)
+        for u in range(2):
+            nc.scalar.copy(out=a_sb[u][:], in_=a_ps[u][:].rearrange("p e j -> p j e"))
+            nc.vector.tensor_tensor(out=top[u][:], in0=b_ps[u][:].rearrange("p e j -> p j e"), in1=a_sb[u][:], op=ALU.max)
+        for t in range(1, PACK):
+            look(t)
+        for u in range(2):
+            for h in range(2):
+                js = slice(HALF * h, HALF * (h + 1))
+                nc.vector.tensor_tensor(
+                    out=hid[h][:, :, 2 * u : 2 * u + 2],
+                    in0=top[u][:, js, :],
+                    in1=gate[u][:, :, js].rearrange("p e j -> p j e"),
+                    op=ALU.mult,
+                )
+
+        hid_codes = [sb.tile([P, HALF], U32, name=f"hid_codes{h}", align_bytes=64) for h in range(2)]
+        hid_scale = [sb.tile([P, HALF], U8, name=f"hid_scale{h}", align_bytes=64) for h in range(2)]
+        for h in range(2):
+            nc.vector.quantize_mx(
+                out=hid_codes[h][:].bitcast(E5M2), scales=hid_scale[h][:], in_=hid[h][:].rearrange("p j t -> p (j t)")
+            )
+        out_by_half = out.rearrange("(g p) j -> p g j", p=P)
+        for h, queue in enumerate((nc.sync, nc.scalar)):
+            y_sb = sb.tile([P, 2, HALF], F32, name=f"y_sb{h}")
+            for g in range(2):
+                y_ps = ps.tile([P, HALF], F32, name=f"y_ps{h}{g}")
+                nc.tensor.matmul_mx(
+                    out=y_ps[:],
+                    lhsT=wb_codes[:, 2 * P * g : 2 * P * (g + 1)].bitcast(E2M1),
+                    lhsT_scale=wb_plane[:, P * g : P * (g + 1)],
+                    rhs=hid_codes[h][:].bitcast(E5M2),
+                    rhs_scale=hid_scale[h][:],
+                    start=True,
+                    stop=True,
+                )
+                if g == 0:
+                    nc.vector.tensor_copy(out=y_sb[:, g, :], in_=y_ps[:])
+                else:
+                    nc.scalar.copy(out=y_sb[:, g, :], in_=y_ps[:])
+            queue.dma_start(out=out_by_half[:, :, HALF * h : HALF * (h + 1)], in_=y_sb[:])

@@ -53,27 +53,43 @@ def tile_list_oneforboth_tablegate_one_plain_kernel(
         offset = sb.tile([P, PACK], F32, name="offset")
         tg_rows = [sb.tile([P, T], F32, name=f"tg_rows{t}", align_bytes=64) for t in range(PACK)]
 
-        for plane in (xt_plane, xo_plane, w_plane, wb_plane):
+        for plane in (w_plane, xo_plane, xt_plane, wb_plane):
             nc.vector.memset(plane[:].bitcast(I32), 0)
 
         tg_by_t = tg.rearrange("(p t) q -> p t q", t=PACK)
+        nc.sync.dma_start(list_o[:], offs2)
+        nc.gpsimd.dma_start(out=slope[:], in_=sg.rearrange("(p t) o -> p (t o)", t=PACK))
+        nc.gpsimd.dma_start(out=offset[:], in_=bg.rearrange("(p t) o -> p (t o)", t=PACK))
         nc.sync.dma_start(list_t[:], offs)
-        nc.sync.dma_start(out=xt_tab[:].bitcast(I32), in_=xt_words[0].bitcast(I32))
-        load_scale_rows(nc.scalar, xt_plane, xt_scales)
+        nc.sync.dma_start(out=w_plane[0:4, :].bitcast(I32), in_=w_scales[0, 0:4, :].bitcast(I32))
+        nc.sync.dma_start(out=w_plane[32:36, :].bitcast(I32), in_=w_scales[0, 4:8, :].bitcast(I32))
+        nc.sync.dma_start(out=w_plane[64:68, :].bitcast(I32), in_=w_scales[0, 8:12, :].bitcast(I32))
+        nc.sync.dma_start(out=w_plane[96:100, :].bitcast(I32), in_=w_scales[0, 12:16, :].bitcast(I32))
         nc.sync.dma_start(out=w_raw[:].bitcast(I32), in_=w_words[0].rearrange("p c r -> p (c r)").bitcast(I32))
         nc.sync.dma_start(out=xo_tab[:].bitcast(I32), in_=xo_words[0].rearrange("p c r -> p (c r)").bitcast(I32))
-        load_scale_rows(nc.scalar, w_plane, w_scales)
-        load_scale_rows(nc.gpsimd, xo_plane, xo_scales)
-        nc.sync.dma_start(list_o[:], offs2)
+        nc.sync.dma_start(out=xo_plane[0:4, :].bitcast(I32), in_=xo_scales[0, 0:4, :].bitcast(I32))
+        nc.sync.dma_start(out=xo_plane[32:36, :].bitcast(I32), in_=xo_scales[0, 4:8, :].bitcast(I32))
+        nc.sync.dma_start(out=xo_plane[64:68, :].bitcast(I32), in_=xo_scales[0, 8:12, :].bitcast(I32))
+        nc.sync.dma_start(out=xo_plane[96:100, :].bitcast(I32), in_=xo_scales[0, 12:16, :].bitcast(I32))
+        nc.sync.dma_start(out=xt_tab[:].bitcast(I32), in_=xt_words[0].bitcast(I32))
         nc.sync.dma_start(out=tg_rows[0][:], in_=tg_by_t[:, 0, :])
-        nc.sync.dma_start(out=tg_rows[1][:], in_=tg_by_t[:, 1, :])
         nc.sync.dma_start(list_g[:], offs3)
-        nc.scalar.dma_start(out=slope[:], in_=sg.rearrange("(p t) o -> p (t o)", t=PACK))
-        nc.scalar.dma_start(out=offset[:], in_=bg.rearrange("(p t) o -> p (t o)", t=PACK))
+        nc.sync.dma_start(out=xt_plane[0:4, :].bitcast(I32), in_=xt_scales[0, 0:4, :].bitcast(I32))
+        nc.sync.dma_start(out=xt_plane[32:36, :].bitcast(I32), in_=xt_scales[0, 4:8, :].bitcast(I32))
+        nc.sync.dma_start(out=xt_plane[64:68, :].bitcast(I32), in_=xt_scales[0, 8:12, :].bitcast(I32))
+        nc.sync.dma_start(out=xt_plane[96:100, :].bitcast(I32), in_=xt_scales[0, 12:16, :].bitcast(I32))
+        nc.sync.dma_start(out=tg_rows[1][:], in_=tg_by_t[:, 1, :])
         nc.sync.dma_start(out=tg_rows[2][:], in_=tg_by_t[:, 2, :])
         nc.sync.dma_start(out=tg_rows[3][:], in_=tg_by_t[:, 3, :])
         nc.sync.dma_start(out=wb_codes[:].bitcast(I32), in_=wb_words[0].bitcast(I32))
-        load_scale_rows(nc.sync, wb_plane, wb_scales)
+        nc.sync.dma_start(out=wb_plane[0:4, :].bitcast(I32), in_=wb_scales[0, 0:4, :].bitcast(I32))
+        nc.sync.dma_start(out=wb_plane[32:36, :].bitcast(I32), in_=wb_scales[0, 4:8, :].bitcast(I32))
+        nc.sync.dma_start(out=wb_plane[64:68, :].bitcast(I32), in_=wb_scales[0, 8:12, :].bitcast(I32))
+        nc.sync.dma_start(out=wb_plane[96:100, :].bitcast(I32), in_=wb_scales[0, 12:16, :].bitcast(I32))
+        zero = sb.tile([P, 1], F32, name="zero")
+        nc.vector.memset(zero[:], 0.0)
+        warm = sb.tile([P, 1], F32, name="warm")
+        nc.scalar.activation(out=warm[:], in_=zero[:], func=ACT.Sigmoid)
 
         xt_codes = sb.tile([P, J], U16, name="xt_codes", align_bytes=64)
         xt_scale = sb.tile([P, J], U8, name="xt_scale", align_bytes=64)
@@ -82,8 +98,6 @@ def tile_list_oneforboth_tablegate_one_plain_kernel(
         w_codes = sb.tile([P, R], U32, name="w_codes", align_bytes=64)
         w_scale = sb.tile([P, R], U8, name="w_scale", align_bytes=64)
 
-        nc.vector.tensor_copy(xt_codes[:], xt_tab[:].indirect(list_t[:]))
-        nc.vector.tensor_copy(xt_scale[:], xt_plane[:].indirect(list_t[:]))
         nc.vector.tensor_copy(
             out=w_codes[:].rearrange("p (t c i) -> p c t i", t=PACK, i=4),
             in_=w_raw[:].rearrange("p (c i t) -> p c t i", t=PACK, i=4),
@@ -94,6 +108,8 @@ def tile_list_oneforboth_tablegate_one_plain_kernel(
         )
         nc.vector.tensor_copy(xo_codes[:], xo_tab[:].indirect(list_o[:]))
         nc.vector.tensor_copy(xo_scale[:], xo_plane[:].indirect(list_o[:]))
+        nc.vector.tensor_copy(xt_codes[:], xt_tab[:].indirect(list_t[:]))
+        nc.vector.tensor_copy(xt_scale[:], xt_plane[:].indirect(list_t[:]))
 
         gate = [sb.tile([P, 2, J], F32, name=f"gate{u}") for u in range(2)]
 
@@ -108,7 +124,7 @@ def tile_list_oneforboth_tablegate_one_plain_kernel(
 
         a_ps = [ps.tile([P, 2, J], F32, name=f"a_ps{u}") for u in range(2)]
         b_ps = [ps.tile([P, 2, J], F32, name=f"b_ps{u}") for u in range(2)]
-        for acc, codes, scale in ((a_ps, xt_codes[:].bitcast(E2M1), xt_scale), (b_ps, xo_codes[:].bitcast(E4M3), xo_scale)):
+        for acc, codes, scale in ((b_ps, xo_codes[:].bitcast(E4M3), xo_scale), (a_ps, xt_codes[:].bitcast(E2M1), xt_scale)):
             for t in range(PACK):
                 cols = slice(P * t, P * (t + 1))
                 nc.tensor.matmul_mx(
@@ -122,13 +138,12 @@ def tile_list_oneforboth_tablegate_one_plain_kernel(
                 )
 
         hid = [sb.tile([P, HALF, PACK], BF16, name=f"hid{h}", align_bytes=64) for h in range(2)]
-        a_sb = [sb.tile([P, J, 2], F32, name=f"a_sb{u}") for u in range(2)]
+        b_sb = [sb.tile([P, J, 2], F32, name=f"b_sb{u}") for u in range(2)]
         top = [sb.tile([P, J, 2], F32, name=f"top{u}") for u in range(2)]
-        look(0)
         for u in range(2):
-            nc.scalar.copy(out=a_sb[u][:], in_=a_ps[u][:].rearrange("p e j -> p j e"))
-            nc.vector.tensor_tensor(out=top[u][:], in0=b_ps[u][:].rearrange("p e j -> p j e"), in1=a_sb[u][:], op=ALU.max)
-        for t in range(1, PACK):
+            nc.scalar.copy(out=b_sb[u][:], in_=b_ps[u][:].rearrange("p e j -> p j e"))
+            nc.vector.tensor_tensor(out=top[u][:], in0=a_ps[u][:].rearrange("p e j -> p j e"), in1=b_sb[u][:], op=ALU.max)
+        for t in range(PACK):
             look(t)
         for u in range(2):
             for h in range(2):

@@ -57,27 +57,27 @@ def tile_list_oneforboth_tablegate_one_plain_kernel(
             nc.vector.memset(plane[:].bitcast(I32), 0)
 
         tg_by_t = tg.rearrange("(p t) q -> p t q", t=PACK)
-        nc.sync.dma_start(list_o[:], offs2)
+        nc.sync.dma_start(out=w_raw[:].bitcast(I32), in_=w_words[0].rearrange("p c r -> p (c r)").bitcast(I32))
         nc.gpsimd.dma_start(out=slope[:], in_=sg.rearrange("(p t) o -> p (t o)", t=PACK))
         nc.gpsimd.dma_start(out=offset[:], in_=bg.rearrange("(p t) o -> p (t o)", t=PACK))
-        nc.sync.dma_start(list_t[:], offs)
+        nc.sync.dma_start(list_o[:], offs2)
         nc.sync.dma_start(out=w_plane[0:4, :].bitcast(I32), in_=w_scales[0, 0:4, :].bitcast(I32))
         nc.sync.dma_start(out=w_plane[32:36, :].bitcast(I32), in_=w_scales[0, 4:8, :].bitcast(I32))
         nc.sync.dma_start(out=w_plane[64:68, :].bitcast(I32), in_=w_scales[0, 8:12, :].bitcast(I32))
         nc.sync.dma_start(out=w_plane[96:100, :].bitcast(I32), in_=w_scales[0, 12:16, :].bitcast(I32))
-        nc.sync.dma_start(out=w_raw[:].bitcast(I32), in_=w_words[0].rearrange("p c r -> p (c r)").bitcast(I32))
         nc.sync.dma_start(out=xo_tab[:].bitcast(I32), in_=xo_words[0].rearrange("p c r -> p (c r)").bitcast(I32))
+        nc.sync.dma_start(list_t[:], offs)
         nc.sync.dma_start(out=xo_plane[0:4, :].bitcast(I32), in_=xo_scales[0, 0:4, :].bitcast(I32))
         nc.sync.dma_start(out=xo_plane[32:36, :].bitcast(I32), in_=xo_scales[0, 4:8, :].bitcast(I32))
         nc.sync.dma_start(out=xo_plane[64:68, :].bitcast(I32), in_=xo_scales[0, 8:12, :].bitcast(I32))
         nc.sync.dma_start(out=xo_plane[96:100, :].bitcast(I32), in_=xo_scales[0, 12:16, :].bitcast(I32))
         nc.sync.dma_start(out=xt_tab[:].bitcast(I32), in_=xt_words[0].bitcast(I32))
         nc.sync.dma_start(out=tg_rows[0][:], in_=tg_by_t[:, 0, :])
-        nc.sync.dma_start(list_g[:], offs3)
         nc.sync.dma_start(out=xt_plane[0:4, :].bitcast(I32), in_=xt_scales[0, 0:4, :].bitcast(I32))
         nc.sync.dma_start(out=xt_plane[32:36, :].bitcast(I32), in_=xt_scales[0, 4:8, :].bitcast(I32))
         nc.sync.dma_start(out=xt_plane[64:68, :].bitcast(I32), in_=xt_scales[0, 8:12, :].bitcast(I32))
         nc.sync.dma_start(out=xt_plane[96:100, :].bitcast(I32), in_=xt_scales[0, 12:16, :].bitcast(I32))
+        nc.sync.dma_start(list_g[:], offs3)
         nc.sync.dma_start(out=tg_rows[1][:], in_=tg_by_t[:, 1, :])
         nc.sync.dma_start(out=tg_rows[2][:], in_=tg_by_t[:, 2, :])
         nc.sync.dma_start(out=tg_rows[3][:], in_=tg_by_t[:, 3, :])

from contextlib import ExitStack

import concourse.mybir as mybir

K, T, J, R, N = 512, 1024, 256, 512, 256
FLOPS = 2 * (2 * K * R * J) + 2 * R * N * J

F32 = mybir.dt.float32
BF16 = mybir.dt.bfloat16
I32 = mybir.dt.int32
U32 = mybir.dt.uint32
U16 = mybir.dt.uint16
U8 = mybir.dt.uint8
E4M3 = mybir.dt.float8_e4m3fn_x4
E5M2 = mybir.dt.float8_e5m2_x4
E2M1 = mybir.dt.float4_e2m1fn_x4
ALU = mybir.AluOpType
ACT = mybir.ActivationFunctionType

P = 128
PACK = 4
HALF = J // 2


def load_scale_rows(queue, plane, scales):
    for q in range(4):
        queue.dma_start(
            out=plane[32 * q : 32 * q + 4, :].bitcast(I32),
            in_=scales[0, 4 * q : 4 * q + 4, :].bitcast(I32),
        )


def tile_list_oneforboth_tablegate_one_plain_kernel(
    tc, xt_words, xt_scales, xo_words, xo_scales, w_words, w_scales, tg, sg, bg, wb_words, wb_scales, offs, offs2, offs3, out
):
    nc = tc.nc
    with ExitStack() as ctx:
        sb = ctx.enter_context(tc.tile_pool(name="sb", bufs=1))
        ps = ctx.enter_context(tc.psum_pool(name="ps", bufs=1))

        list_t = sb.tile([P, J // 16], U16, name="list_t")
        list_o = sb.tile([P, J // 16], U16, name="list_o")
        list_g = sb.tile([P, J // 16], U16, name="list_g")
        xt_tab = sb.tile([P, T], U16, name="xt_tab", align_bytes=64)
        xo_tab = sb.tile([P, T], U32, name="xo_tab", align_bytes=64)
        xt_plane = sb.tile([P, T], U8, name="xt_plane", align_bytes=64)
        xo_plane = sb.tile([P, T], U8, name="xo_plane", align_bytes=64)
        w_raw = sb.tile([P, R], U32, name="w_raw", align_bytes=64)
        w_plane = sb.tile([P, R], U8, name="w_plane", align_bytes=64)
        wb_codes = sb.tile([P, 2 * N], U8, name="wb_codes", align_bytes=64)
        wb_plane = sb.tile([P, N], U8, name="wb_plane", align_bytes=64)
        slope = sb.tile([P, PACK], F32, name="slope")
        offset = sb.tile([P, PACK], F32, name="offset")
        tg_rows = [sb.tile([P, T], F32, name=f"tg_rows{t}", align_bytes=64) for t in range(PACK)]

        for plane in (w_plane, xo_plane, xt_plane, wb_plane):
            nc.vector.memset(plane[:].bitcast(I32), 0)

        tg_by_t = tg.rearrange("(p t) q -> p t q", t=PACK)
        nc.sync.dma_start(out=w_raw[:].bitcast(I32), in_=w_words[0].rearrange("p c r -> p (c r)").bitcast(I32))
        nc.gpsimd.dma_start(out=slope[:], in_=sg.rearrange("(p t) o -> p (t o)", t=PACK))
        nc.gpsimd.dma_start(out=offset[:], in_=bg.rearrange("(p t) o -> p (t o)", t=PACK))
        nc.sync.dma_start(list_o[:], offs2)
        nc.sync.dma_start(out=w_plane[0:4, :].bitcast(I32), in_=w_scales[0, 0:4, :].bitcast(I32))
        nc.sync.dma_start(out=w_plane[32:36, :].bitcast(I32), in_=w_scales[0, 4:8, :].bitcast(I32))
        nc.sync.dma_start(out=w_plane[64:68, :].bitcast(I32), in_=w_scales[0, 8:12, :].bitcast(I32))
        nc.sync.dma_start(out=w_plane[96:100, :].bitcast(I32), in_=w_scales[0, 12:16, :].bitcast(I32))
        nc.sync.dma_start(out=xo_tab[:].bitcast(I32), in_=xo_words[0].rearrange("p c r -> p (c r)").bitcast(I32))
        nc.sync.dma_start(list_t[:], offs)
        nc.sync.dma_start(out=xo_plane[0:4, :].bitcast(I32), in_=xo_scales[0, 0:4, :].bitcast(I32))
        nc.sync.dma_start(out=xo_plane[32:36, :].bitcast(I32), in_=xo_scales[0, 4:8, :].bitcast(I32))
        nc.sync.dma_start(out=xo_plane[64:68, :].bitcast(I32), in_=xo_scales[0, 8:12, :].bitcast(I32))
        nc.sync.dma_start(out=xo_plane[96:100, :].bitcast(I32), in_=xo_scales[0, 12:16, :].bitcast(I32))
        nc.sync.dma_start(out=xt_tab[:].bitcast(I32), in_=xt_words[0].bitcast(I32))
        nc.sync.dma_start(out=tg_rows[0][:], in_=tg_by_t[:, 0, :])
        nc.sync.dma_start(out=xt_plane[0:4, :].bitcast(I32), in_=xt_scales[0, 0:4, :].bitcast(I32))
        nc.sync.dma_start(out=xt_plane[32:36, :].bitcast(I32), in_=xt_scales[0, 4:8, :].bitcast(I32))
        nc.sync.dma_start(out=xt_plane[64:68, :].bitcast(I32), in_=xt_scales[0, 8:12, :].bitcast(I32))
        nc.sync.dma_start(out=xt_plane[96:100, :].bitcast(I32), in_=xt_scales[0, 12:16, :].bitcast(I32))
        nc.sync.dma_start(list_g[:], offs3)
        nc.sync.dma_start(out=tg_rows[1][:], in_=tg_by_t[:, 1, :])
        nc.sync.dma_start(out=tg_rows[2][:], in_=tg_by_t[:, 2, :])
        nc.sync.dma_start(out=tg_rows[3][:], in_=tg_by_t[:, 3, :])
        nc.sync.dma_start(out=wb_codes[:].bitcast(I32), in_=wb_words[0].bitcast(I32))
        nc.sync.dma_start(out=wb_plane[0:4, :].bitcast(I32), in_=wb_scales[0, 0:4, :].bitcast(I32))
        nc.sync.dma_start(out=wb_plane[32:36, :].bitcast(I32), in_=wb_scales[0, 4:8, :].bitcast(I32))
        nc.sync.dma_start(out=wb_plane[64:68, :].bitcast(I32), in_=wb_scales[0, 8:12, :].bitcast(I32))
        nc.sync.dma_start(out=wb_plane[96:100, :].bitcast(I32), in_=wb_scales[0, 12:16, :].bitcast(I32))
        zero = sb.tile([P, 1], F32, name="zero")
        nc.vector.memset(zero[:], 0.0)
        warm = sb.tile([P, 1], F32, name="warm")
        nc.scalar.activation(out=warm[:], in_=zero[:], func=ACT.Sigmoid)

        xt_codes = sb.tile([P, J], U16, name="xt_codes", align_bytes=64)
        xt_scale = sb.tile([P, J], U8, name="xt_scale", align_bytes=64)
        xo_codes = sb.tile([P, J], U32, name="xo_codes", align_bytes=64)
        xo_scale = sb.tile([P, J], U8, name="xo_scale", align_bytes=64)
        w_codes = sb.tile([P, R], U32, name="w_codes", align_bytes=64)
        w_scale = sb.tile([P, R], U8, name="w_scale", align_bytes=64)

        nc.vector.tensor_copy(
            out=w_codes[:].rearrange("p (t c i) -> p c t i", t=PACK, i=4),
            in_=w_raw[:].rearrange("p (c i t) -> p c t i", t=PACK, i=4),
        )
        nc.vector.tensor_copy(
            out=w_scale[:].rearrange("p (t c i) -> p c t i", t=PACK, i=16),
            in_=w_plane[:].rearrange("p (c i t) -> p c t i", t=PACK, i=16),
        )
        nc.vector.tensor_copy(xo_codes[:], xo_tab[:].indirect(list_o[:]))
        nc.vector.tensor_copy(xo_scale[:], xo_plane[:].indirect(list_o[:]))
        nc.vector.tensor_copy(xt_codes[:], xt_tab[:].indirect(list_t[:]))
        nc.vector.tensor_copy(xt_scale[:], xt_plane[:].indirect(list_t[:]))

        gate = [sb.tile([P, 2, J], F32, name=f"gate{u}") for u in range(2)]

        def look(t):
            nc.scalar.activation(
                out=gate[t // 2][:, t % 2, :],
                in_=tg_rows[t][:].indirect(list_g[:]),
                func=ACT.Sigmoid,
                bias=offset[:, t : t + 1],
                scale=slope[:, t : t + 1],
            )

        a_ps = [ps.tile([P, 2, J], F32, name=f"a_ps{u}") for u in range(2)]
        b_ps = [ps.tile([P, 2, J], F32, name=f"b_ps{u}") for u in range(2)]
        for acc, codes, scale in ((b_ps, xo_codes[:].bitcast(E4M3), xo_scale), (a_ps, xt_codes[:].bitcast(E2M1), xt_scale)):
            for t in range(PACK):
                cols = slice(P * t, P * (t + 1))
                nc.tensor.matmul_mx(
                    out=acc[t // 2][:, t % 2, :],
                    lhsT=w_codes[:, cols].bitcast(E4M3),
                    lhsT_scale=w_scale[:, cols],
                    rhs=codes,
                    rhs_scale=scale[:],
                    start=True,
                    stop=True,
                )

        hid = [sb.tile([P, HALF, PACK], BF16, name=f"hid{h}", align_bytes=64) for h in range(2)]
        b_sb = [sb.tile([P, J, 2], F32, name=f"b_sb{u}") for u in range(2)]
        top = [sb.tile([P, J, 2], F32, name=f"top{u}") for u in range(2)]
        for u in range(2):
            nc.scalar.copy(out=b_sb[u][:], in_=b_ps[u][:].rearrange("p e j -> p j e"))
            nc.vector.tensor_tensor(out=top[u][:], in0=a_ps[u][:].rearrange("p e j -> p j e"), in1=b_sb[u][:], op=ALU.max)
        for t in range(PACK):
            look(t)
        for u in range(2):
            for h in range(2):
                js = slice(HALF * h, HALF * (h + 1))
                nc.vector.tensor_tensor(
                    out=hid[h][:, :, 2 * u : 2 * u + 2],
                    in0=top[u][:, js, :],
                    in1=gate[u][:, :, js].rearrange("p e j -> p j e"),
                    op=ALU.mult,
                )

        hid_codes = [sb.tile([P, HALF], U32, name=f"hid_codes{h}", align_bytes=64) for h in range(2)]
        hid_scale = [sb.tile([P, HALF], U8, name=f"hid_scale{h}", align_bytes=64) for h in range(2)]
        for h in range(2):
            nc.vector.quantize_mx(
                out=hid_codes[h][:].bitcast(E5M2), scales=hid_scale[h][:], in_=hid[h][:].rearrange("p j t -> p (j t)")
            )
        out_by_half = out.rearrange("(g p) j -> p g j", p=P)
        for h, queue in enumerate((nc.sync, nc.scalar)):
            y_sb = sb.tile([P, 2, HALF], F32, name=f"y_sb{h}")
            for g in range(2):
                y_ps = ps.tile([P, HALF], F32, name=f"y_ps{h}{g}")
                nc.tensor.matmul_mx(
                    out=y_ps[:],
                    lhsT=wb_codes[:, 2 * P * g : 2 * P * (g + 1)].bitcast(E2M1),
                    lhsT_scale=wb_plane[:, P * g : P * (g + 1)],
                    rhs=hid_codes[h][:].bitcast(E5M2),
                    rhs_scale=hid_scale[h][:],
                    start=True,
                    stop=True,
                )
                if g == 0:
                    nc.vector.tensor_copy(out=y_sb[:, g, :], in_=y_ps[:])
                else:
                    nc.scalar.copy(out=y_sb[:, g, :], in_=y_ps[:])
            queue.dma_start(out=out_by_half[:, :, HALF * h : HALF * (h + 1)], in_=y_sb[:])
